import numpy as np
import ml_dtypes


def mxq(x, axis, fmt="e4m3"):
    dtype, down = {"e4m3": (ml_dtypes.float8_e4m3fn, 7), "e5m2": (ml_dtypes.float8_e5m2, 14)}[fmt]
    v = np.moveaxis(np.asarray(x, np.float32).astype(ml_dtypes.bfloat16).astype(np.float64), axis, -1)
    blocks = v.reshape(v.shape[:-1] + (-1, 32))
    amax = np.abs(blocks).max(-1, keepdims=True)
    byte = np.maximum(np.where(amax > 0, np.frexp(amax)[1] - 1 + 127, 0) - down, 1)
    scale = np.exp2(byte - 127.0)
    codes = (blocks / scale).astype(np.float32).astype(dtype).astype(np.float64)
    return np.moveaxis((codes * scale).reshape(v.shape), -1, axis)


WIDE = False


def mx_kscale(k):
    if not WIDE:
        return np.ones(k)
    levels = np.array([10, -10, 5, -5, 0])
    if k % 512:
        return np.exp2(np.random.permutation(np.resize(levels, k // 32))).repeat(32)
    a = np.empty((k // 512, 16))
    for p in range(k // 512):
        a[p, :8] = np.random.permutation(np.resize(levels, 8))
        for g in range(8):
            far = levels[np.abs(levels - a[p, g]) >= 10]
            a[p, g + 8] = far[np.random.randint(len(far))]
    return np.exp2(a.ravel()).repeat(32)


def f64(x):
    return np.asarray(x).astype(np.float64)


def striped(idx):
    return np.tile(np.asarray(idx).reshape(-1, 16).T, (8, 1)).astype(np.uint16)


def unstriped(offs):
    return offs[:16].T.reshape(-1).astype(np.int64)


E2M1 = np.array([0.0, 0.5, 1.0, 1.5, 2.0, 3.0, 4.0, 6.0, -0.0, -0.5, -1.0, -1.5, -2.0, -3.0, -4.0, -6.0])


def pack_weight(w, fmt):
    k, n = w.shape
    w = f64(np.asarray(w, np.float32).astype(ml_dtypes.bfloat16)).reshape(k // 32, 32, n)
    amax = np.abs(w).max(1)
    if fmt == "e4m3":
        byte = np.frexp(amax)[1] - 1 + 127 - 7
    else:
        mant, ex = np.frexp(amax / 6.0)
        byte = np.where(mant > 0.5, ex, ex - 1) + 127
    byte = np.clip(np.where(amax > 0, byte, 1), 1, 254)
    scaled = (w * np.exp2(127.0 - byte)[:, None, :]).reshape(k, n).astype(np.float32)
    by_word = np.ascontiguousarray(scaled.reshape(k // 512, 128, 4, n).transpose(0, 1, 3, 2))
    if fmt == "e4m3":
        words = by_word.astype(ml_dtypes.float8_e4m3fn).view(np.uint8)
    else:
        c = by_word.astype(ml_dtypes.float4_e2m1fn).view(np.uint8) & 0xF
        words = (c[..., 0::2] | (c[..., 1::2] << 4)).reshape(k // 512, 128, 2 * n)
    return np.ascontiguousarray(words), np.ascontiguousarray(byte.astype(np.uint8).reshape(k // 512, 16, n))


def unpack_weight(words, scales, fmt):
    g, _, n = scales.shape
    words = np.ascontiguousarray(words).reshape(g, 128, n, -1)
    if fmt == "e4m3":
        vals = words.view(ml_dtypes.float8_e4m3fn).astype(np.float64)
    else:
        nib = np.empty((g, 128, n, 4), np.uint8)
        nib[..., 0::2] = words & 0xF
        nib[..., 1::2] = words >> 4
        vals = E2M1[nib]
    vals = vals * np.repeat(np.exp2(scales.astype(np.float64) - 127.0), 8, axis=1)[..., None]
    return vals.transpose(0, 1, 3, 2).reshape(g * 512, n)


def softplus(v):
    return np.log(1.0 + np.exp(v))


def sigmoid(v):
    return 1.0 / (1.0 + np.exp(-v))


D, K, R, T, I, Q = 512, 512, 512, 2048, 512, 128


def setup_inputs():
    n = np.random.standard_normal
    idx = np.random.permutation(T)[:I]
    fd = mx_kscale(D)
    fk = mx_kscale(K)
    fr = mx_kscale(R)
    keysp = pack_weight(n((D, T)) / fd[:, None], "e4m3")
    tabp = pack_weight(n((K, T)) / fk[:, None], "e4m3")
    return {
        "query": (n((D, Q)) * 0.9 / np.sqrt(D) * fd[:, None]).astype(np.float32),
        "keys_words": keysp[0],
        "keys_scales": keysp[1],
        "th": (np.random.uniform(-0.3, 0.6, (Q, 1))).astype(np.float32),
        "reserve": (np.random.uniform(50.0, 200.0, (Q, 1))).astype(np.float32),
        "tab_words": tabp[0],
        "tab_scales": tabp[1],
        "w1": (n((K, R)) * 1 / np.sqrt(K) * fk[:, None]).astype(np.float32),
        "gain": (np.random.uniform(0.5, 2.0, (R, 1))).astype(np.float32),
        "gout": (n((R, Q)) * 1 / np.sqrt(R) * fr[:, None]).astype(np.float32),
        "hsc": (np.random.uniform(0.7, 1.4, (R, 1)) / fr[:, None]).astype(np.float32),
        "old": (0.5 * n((Q, T))).astype(np.float32),
        "offs": striped(idx),
    }


def reference(query, keys_words, keys_scales, th, reserve, tab_words, tab_scales, w1, gain, gout, hsc, old, offs):
    idx = unstriped(offs)
    keysu = unpack_weight(keys_words, keys_scales, "e4m3")
    tabu = unpack_weight(tab_words, tab_scales, "e4m3")
    queryq = mxq(f64(query), 0, "e4m3")
    keysidxg = keysu[:, idx]
    a = queryq.T @ keysidxg
    p = softplus(a - f64(th))
    z = np.sum(p, axis=1, keepdims=True) + f64(reserve)
    w1q = mxq(f64(w1), 0, "e4m3")
    tabidxg = tabu[:, idx]
    zh = w1q.T @ tabidxg
    ht = np.tanh(zh)
    hv = ht * f64(gain)
    hs1 = hv * f64(hsc)
    goutq = mxq(f64(gout), 0, "e4m3")
    hs1q = mxq(hs1, 0, "e4m3")
    c0 = goutq.T @ hs1q
    dz = np.sum(c0 * p / np.square(z) * (-1.0), axis=1, keepdims=True)
    dp = c0 / z + dz
    da = dp * sigmoid(a - f64(th))
    gs = da * 512.0
    gf = np.zeros((Q, T))
    gf[:, idx] = gs
    y = f64(old) + gf
    return y

@@ -1,0 +1,236 @@
+from contextlib import ExitStack
+
+import concourse.mybir as mybir
+
+D, K, R, T, I, Q = 512, 512, 512, 2048, 512, 128
+FLOPS = 2 * (D * Q * I + K * R * I + R * Q * I)
+
+F32 = mybir.dt.float32
+BF16 = mybir.dt.bfloat16
+I32 = mybir.dt.int32
+U32 = mybir.dt.uint32
+U16 = mybir.dt.uint16
+U8 = mybir.dt.uint8
+FP8X4 = mybir.dt.float8_e4m3fn_x4
+ALU = mybir.AluOpType
+ACT = mybir.ActivationFunctionType
+
+P = 128
+PACK = 4
+HALF = I // 2
+CHUNK = 128
+OUT_SCALE = 512.0
+LN_FLOOR = 2.0 ** -60
+STORE_COLS = 512
+
+
+def tile_attend_blrgained_capped_kernel(
+    tc, query, keys_words, keys_scales, th, reserve, tab_words, tab_scales, w1, gain, gout, hsc, old, offs, out
+):
+    nc = tc.nc
+    with ExitStack() as ctx:
+        sb = ctx.enter_context(tc.tile_pool(name="sb", bufs=1))
+        ps = ctx.enter_context(tc.psum_pool(name="ps", bufs=1))
+
+        def load_scale_rows(engine, plane, scales):
+            rows = scales[0].rearrange("(g f) c -> f g c", f=4)
+            for f in range(4):
+                engine.dma_start(out=plane[f:P:32, :].bitcast(I32), in_=rows[f].bitcast(I32))
+
+        def words_view(words):
+            return words[0].rearrange("p n t -> p (n t)").bitcast(I32)
+
+        def quantize(name, grouped, width):
+            codes = sb.tile([P, width], U32, name=name + "_codes", align_bytes=64)
+            plane = sb.tile([P, width], U8, name=name + "_plane", align_bytes=64)
+            nc.vector.quantize_mx(out=codes[:].bitcast(FP8X4), scales=plane[:], in_=grouped)
+            return codes, plane
+
+        def product(acc, lhs, lhs_cols, rhs_codes, rhs_plane):
+            nc.tensor.matmul_mx(
+                out=acc,
+                lhsT=lhs[0][:, lhs_cols].bitcast(FP8X4),
+                lhsT_scale=lhs[1][:, lhs_cols],
+                rhs=rhs_codes.bitcast(FP8X4),
+                rhs_scale=rhs_plane,
+                start=True,
+                stop=True,
+            )
+
+        offsets = sb.tile([P, I // 16], U16, name="offsets")
+        tab_pool_plane = sb.tile([P, T], U8, name="tab_pool_plane", tag="tab_plane_then_keys")
+        keys_pool_plane = sb.tile([P, T], U8, name="keys_pool_plane", tag="keys_plane_then_gout")
+        gf = sb.tile([P, T], F32, name="gf")
+        warm = sb.tile([P, 1], F32, name="warm")
+        warm_out = sb.tile([P, 1], F32, name="warm_out", tag="warm_then_query")
+        nc.vector.memset(tab_pool_plane[:].bitcast(I32), 0)
+        nc.vector.memset(warm[:], 0.0)
+        nc.gpsimd.memset(keys_pool_plane[:].bitcast(I32), 0)
+        nc.vector.memset(gf[:], 0.0)
+        nc.scalar.activation(out=warm_out[:], in_=warm[:], func=ACT.Sigmoid)
+
+        w1_rows = w1.rearrange("(p j) r -> p j r", j=PACK)
+        w1_raw = [sb.tile([P, PACK, R // 2], F32, name="w1_raw%d" % h, tag="w1_then_old%d" % h) for h in range(2)]
+        tab_pool = sb.tile([P, T], U32, name="tab_pool")
+        query_raw = sb.tile([P, PACK, Q], F32, name="query_raw", tag="warm_then_query")
+        nc.sync.dma_start(offsets[:], offs)
+        nc.sync.dma_start(out=w1_raw[0][:], in_=w1_rows[:, :, 0 : R // 2])
+        load_scale_rows(nc.scalar, tab_pool_plane, tab_scales)
+        nc.sync.dma_start(out=w1_raw[1][:], in_=w1_rows[:, :, R // 2 : R])
+        nc.sync.dma_start(out=tab_pool[:].bitcast(I32), in_=words_view(tab_words))
+        nc.sync.dma_start(out=query_raw[:], in_=query.rearrange("(p j) q -> p j q", j=PACK))
+
+        gain_sb = sb.tile([P, PACK], F32, name="gain_sb")
+        hsc_sb = sb.tile([P, PACK], F32, name="hsc_sb")
+        th_sb = sb.tile([P, 1], F32, name="th_sb")
+        reserve_sb = sb.tile([P, 1], F32, name="reserve_sb")
+        load_scale_rows(nc.gpsimd, keys_pool_plane, keys_scales)
+        nc.gpsimd.dma_start(out=gain_sb[:], in_=gain.rearrange("(p j) o -> p (j o)", j=PACK))
+        nc.gpsimd.dma_start(out=hsc_sb[:], in_=hsc.rearrange("(p j) o -> p (j o)", j=PACK))
+        nc.gpsimd.dma_start(out=th_sb[:], in_=th)
+        nc.gpsimd.dma_start(out=reserve_sb[:], in_=reserve)
+
+        w1_grouped = sb.tile([P, PACK, P, PACK], BF16, name="w1_grouped", align_bytes=64)
+        dealt = w1_grouped[:].rearrange("p t m j -> p m t j")
+        w1_src = [w1_raw[h][:].rearrange("p j (m t) -> p m t j", t=PACK) for h in range(2)]
+        nc.scalar.copy(out=dealt[:, 0 : P // 2], in_=w1_src[0])
+
+        tab_plane = sb.tile([P, I], U8, name="tab_plane", align_bytes=64)
+        nc.vector.tensor_copy(out=tab_plane[:], in_=tab_pool_plane[:].indirect(offsets[:]))
+        keys_pool = sb.tile([P, T], U32, name="keys_pool", tag="tab_plane_then_keys")
+        nc.sync.dma_start(out=keys_pool[:].bitcast(I32), in_=words_view(keys_words))
+        nc.vector.tensor_copy(out=dealt[:, P // 2 : P], in_=w1_src[1])
+        w1_mx = quantize("w1", w1_grouped[:].rearrange("p t m j -> p (t m j)"), R)
+        keys_plane = sb.tile([P, I], U8, name="keys_plane", align_bytes=64)
+        nc.vector.tensor_copy(out=keys_plane[:], in_=keys_pool_plane[:].indirect(offsets[:]))
+        gout_raw = sb.tile([P, PACK, Q], F32, name="gout_raw", tag="keys_plane_then_gout")
+        nc.sync.dma_start(out=gout_raw[:], in_=gout.rearrange("(p j) q -> p j q", j=PACK))
+        old_sb = [sb.tile([P, T // 2], F32, name="old_sb%d" % h, tag="w1_then_old%d" % h) for h in range(2)]
+        for h in range(2):
+            nc.sync.dma_start(out=old_sb[h][:], in_=old[:, h * (T // 2) : (h + 1) * (T // 2)])
+
+        def gather_half(name, pool, h):
+            codes = sb.tile([P, HALF], U32, name="%s_codes%d" % (name, h), align_bytes=64)
+            cols = HALF // 16
+            nc.vector.tensor_copy(out=codes[:], in_=pool[:].indirect(offsets[:, h * cols : (h + 1) * cols]))
+            return codes
+
+        tab_codes = [gather_half("tab", tab_pool, h) for h in range(2)]
+
+        feature_scale = sb.tile([P, PACK], F32, name="feature_scale")
+        nc.vector.tensor_tensor(out=feature_scale[:], in0=gain_sb[:], in1=hsc_sb[:], op=ALU.mult)
+
+        query_grouped = sb.tile([P, Q, PACK], BF16, name="query_grouped", align_bytes=64)
+        nc.scalar.activation(
+            out=query_grouped[:], in_=query_raw[:].rearrange("p j q -> p q j"), func=ACT.Copy, scale=-1.0
+        )
+
+        n_chunks = I // CHUNK
+        ht = []
+        for c in range(n_chunks):
+            h, lo = divmod(c * CHUNK, HALF)
+            zh = ps.tile([P, PACK, CHUNK], F32, name="zh%d" % c)
+            for t in range(PACK):
+                product(
+                    zh[:, t, :], w1_mx, slice(t * P, (t + 1) * P),
+                    tab_codes[h][:, lo : lo + CHUNK], tab_plane[:, c * CHUNK : (c + 1) * CHUNK],
+                )
+            ht_c = sb.tile([P, CHUNK, PACK], F32, name="ht%d" % c)
+            nc.scalar.activation(out=ht_c[:], in_=zh[:].rearrange("p t i -> p i t"), func=ACT.Tanh)
+            ht.append(ht_c)
+
+        query_mx = quantize("query", query_grouped[:].rearrange("p q j -> p (q j)"), Q)
+
+        hs1 = [sb.tile([P, CHUNK, PACK], BF16, name="hs1_%d" % c, align_bytes=64) for c in range(n_chunks)]
+
+        def scale_features(c):
+            nc.vector.tensor_tensor(
+                out=hs1[c][:], in0=ht[c][:], in1=feature_scale[:].unsqueeze(1).to_broadcast([P, CHUNK, PACK]), op=ALU.mult
+            )
+
+        scale_features(0)
+        keys_codes = [gather_half("keys", keys_pool, h) for h in range(2)]
+
+        neg_a = [ps.tile([P, HALF], F32, name="neg_a%d" % h) for h in range(2)]
+        sig_neg = sb.tile([P, I], F32, name="sig_neg")
+        for h in range(2):
+            cols = slice(h * HALF, (h + 1) * HALF)
+            product(neg_a[h][:], query_mx, slice(0, Q), keys_codes[h][:], keys_plane[:, cols])
+            nc.scalar.activation(out=sig_neg[:, cols], in_=neg_a[h][:], func=ACT.Sigmoid, bias=th_sb[:])
+
+        gout_grouped = sb.tile([P, Q, PACK], BF16, name="gout_grouped", align_bytes=64)
+        nc.vector.tensor_copy(out=gout_grouped[:], in_=gout_raw[:].rearrange("p j q -> p q j"))
+        scale_features(1)
+        gout_mx = quantize("gout", gout_grouped[:].rearrange("p q j -> p (q j)"), Q)
+
+        c0 = [ps.tile([P, HALF], F32, name="c0_%d" % h) for h in range(2)]
+
+        def read_gradient(c):
+            h, lo = divmod(c * CHUNK, HALF)
+            codes, plane = quantize("hs1_%d" % c, hs1[c][:].rearrange("p i t -> p (i t)"), CHUNK)
+            product(c0[h][:, lo : lo + CHUNK], gout_mx, slice(0, Q), codes[:], plane[:])
+
+        read_gradient(0)
+        for c in range(2, n_chunks):
+            scale_features(c)
+            read_gradient(c - 1)
+        read_gradient(n_chunks - 1)
+
+        ln_sig = sb.tile([P, I], F32, name="ln_sig")
+        neg_p = sb.tile([P, I], F32, name="neg_p")
+        neg_p_sum = [sb.tile([P, 1], F32, name="neg_p_sum%d" % h) for h in range(2)]
+        for h in range(2):
+            cols = slice(h * HALF, (h + 1) * HALF)
+            nc.scalar.activation(out=ln_sig[:, cols], in_=sig_neg[:, cols], func=ACT.Ln, bias=LN_FLOOR)
+            nc.vector.scalar_tensor_tensor(
+                out=neg_p[:, cols], in0=neg_a[h][:], scalar=th_sb[:], in1=ln_sig[:, cols],
+                op0=ALU.add, op1=ALU.min, accum_out=neg_p_sum[h][:],
+            )
+        neg_slope = sb.tile([P, I], F32, name="neg_slope")
+        nc.scalar.activation(out=neg_slope[:], in_=sig_neg[:], func=ACT.Copy, scale=OUT_SCALE, bias=-OUT_SCALE)
+
+        neg_z = sb.tile([P, 1], F32, name="neg_z")
+        neg_rz = sb.tile([P, 1], F32, name="neg_rz")
+        neg_rz2 = sb.tile([P, 1], F32, name="neg_rz2")
+        neg_dz = sb.tile([P, 1], F32, name="neg_dz")
+        weighted = sb.tile([P, I], F32, name="weighted")
+        weighted_sum = [sb.tile([P, 1], F32, name="weighted_sum%d" % h) for h in range(2)]
+
+        def weigh(h):
+            cols = slice(h * HALF, (h + 1) * HALF)
+            nc.vector.scalar_tensor_tensor(
+                out=weighted[:, cols], in0=c0[h][:], scalar=1.0, in1=neg_p[:, cols],
+                op0=ALU.mult, op1=ALU.mult, accum_out=weighted_sum[h][:],
+            )
+
+        nc.vector.tensor_scalar(
+            out=neg_z[:], in0=neg_p_sum[0][:], scalar1=neg_p_sum[1][:], scalar2=reserve_sb[:], op0=ALU.add, op1=ALU.subtract
+        )
+        weigh(0)
+        nc.vector.reciprocal(out=neg_rz[:], in_=neg_z[:])
+        nc.vector.tensor_scalar(
+            out=neg_rz2[:], in0=neg_rz[:], scalar1=neg_rz[:], scalar2=-1.0, op0=ALU.mult, op1=ALU.mult
+        )
+        weigh(1)
+        nc.vector.tensor_scalar(
+            out=neg_dz[:], in0=weighted_sum[0][:], scalar1=weighted_sum[1][:], scalar2=neg_rz2[:], op0=ALU.add, op1=ALU.mult
+        )
+
+        neg_dp = [sb.tile([P, HALF], F32, name="neg_dp%d" % h) for h in range(2)]
+        nc.vector.tensor_scalar(
+            out=neg_dp[0][:], in0=c0[0][:], scalar1=neg_rz[:], scalar2=neg_dz[:], op0=ALU.mult, op1=ALU.add
+        )
+        nc.scalar.activation(out=neg_dp[1][:], in_=c0[1][:], func=ACT.Identity, scale=neg_rz[:], bias=neg_dz[:])
+        for h in range(2):
+            cols = HALF // 16
+            nc.vector.tensor_tensor(
+                out=gf[:].indirect(offsets[:, h * cols : (h + 1) * cols]),
+                in0=neg_dp[h][:], in1=neg_slope[:, h * HALF : (h + 1) * HALF], op=ALU.mult,
+            )
+
+        for lo in range(0, T, STORE_COLS):
+            cols = slice(lo, lo + STORE_COLS)
+            h, at = divmod(lo, T // 2)
+            total = sb.tile([P, STORE_COLS], F32, name="total%d" % lo)
+            nc.vector.tensor_tensor(out=total[:], in0=gf[:, cols], in1=old_sb[h][:, at : at + STORE_COLS], op=ALU.add)
+            nc.sync.dma_start(out=out[:, cols], in_=total[:])

@@ -58,56 +58,64 @@ def tile_attend_blrgained_capped_kernel(
             )
 
         offsets = sb.tile([P, I // 16], U16, name="offsets")
-        tab_pool_plane = sb.tile([P, T], U8, name="tab_pool_plane", tag="tab_plane_then_keys")
-        keys_pool_plane = sb.tile([P, T], U8, name="keys_pool_plane", tag="keys_plane_then_gout")
+        tab_pool_plane = sb.tile([P, T], U8, name="tab_pool_plane")
+        keys_pool_plane = sb.tile([P, T], U8, name="keys_pool_plane")
         gf = sb.tile([P, T], F32, name="gf")
-        warm = sb.tile([P, 1], F32, name="warm")
-        warm_out = sb.tile([P, 1], F32, name="warm_out", tag="warm_then_query")
-        nc.vector.memset(tab_pool_plane[:].bitcast(I32), 0)
-        nc.vector.memset(warm[:], 0.0)
-        nc.gpsimd.memset(keys_pool_plane[:].bitcast(I32), 0)
-        nc.vector.memset(gf[:], 0.0)
-        nc.scalar.activation(out=warm_out[:], in_=warm[:], func=ACT.Sigmoid)
-
         w1_rows = w1.rearrange("(p j) r -> p j r", j=PACK)
-        w1_raw = [sb.tile([P, PACK, R // 2], F32, name="w1_raw%d" % h, tag="w1_then_old%d" % h) for h in range(2)]
+        w1_raw = [sb.tile([P, PACK, R // 2], F32, name="w1_raw%d" % h) for h in range(2)]
         tab_pool = sb.tile([P, T], U32, name="tab_pool")
-        query_raw = sb.tile([P, PACK, Q], F32, name="query_raw", tag="warm_then_query")
         nc.sync.dma_start(offsets[:], offs)
-        nc.sync.dma_start(out=w1_raw[0][:], in_=w1_rows[:, :, 0 : R // 2])
-        load_scale_rows(nc.scalar, tab_pool_plane, tab_scales)
-        nc.sync.dma_start(out=w1_raw[1][:], in_=w1_rows[:, :, R // 2 : R])
+        for h in range(2):
+            nc.sync.dma_start(out=w1_raw[h][:], in_=w1_rows[:, :, h * (R // 2) : (h + 1) * (R // 2)])
         nc.sync.dma_start(out=tab_pool[:].bitcast(I32), in_=words_view(tab_words))
-        nc.sync.dma_start(out=query_raw[:], in_=query.rearrange("(p j) q -> p j q", j=PACK))
+        nc.vector.memset(tab_pool_plane[:].bitcast(I32), 0)
+        load_scale_rows(nc.scalar, tab_pool_plane, tab_scales)
 
         gain_sb = sb.tile([P, PACK], F32, name="gain_sb")
         hsc_sb = sb.tile([P, PACK], F32, name="hsc_sb")
         th_sb = sb.tile([P, 1], F32, name="th_sb")
         reserve_sb = sb.tile([P, 1], F32, name="reserve_sb")
-        load_scale_rows(nc.gpsimd, keys_pool_plane, keys_scales)
         nc.gpsimd.dma_start(out=gain_sb[:], in_=gain.rearrange("(p j) o -> p (j o)", j=PACK))
         nc.gpsimd.dma_start(out=hsc_sb[:], in_=hsc.rearrange("(p j) o -> p (j o)", j=PACK))
         nc.gpsimd.dma_start(out=th_sb[:], in_=th)
         nc.gpsimd.dma_start(out=reserve_sb[:], in_=reserve)
 
-        w1_grouped = sb.tile([P, PACK, P, PACK], BF16, name="w1_grouped", align_bytes=64)
-        dealt = w1_grouped[:].rearrange("p t m j -> p m t j")
-        w1_src = [w1_raw[h][:].rearrange("p j (m t) -> p m t j", t=PACK) for h in range(2)]
-        nc.scalar.copy(out=dealt[:, 0 : P // 2], in_=w1_src[0])
+        with tc.tile_pool(name="head", bufs=1) as head:
+            warm = head.tile([P, 1], F32, name="warm")
+            warm_out = head.tile([P, 1], F32, name="warm_out")
+            nc.vector.memset(warm[:], 0.0)
+            nc.scalar.activation(out=warm_out[:], in_=warm[:], func=ACT.Sigmoid)
 
+        late = ctx.enter_context(tc.tile_pool(name="late", bufs=1))
+        query_raw = late.tile([P, PACK, Q], F32, name="query_raw")
+        keys_pool = late.tile([P, T], U32, name="keys_pool")
+        gout_raw = late.tile([P, PACK, Q], F32, name="gout_raw")
+        old_sb = late.tile([P, T], F32, name="old_sb")
+        nc.sync.dma_start(out=query_raw[:], in_=query.rearrange("(p j) q -> p j q", j=PACK))
+        nc.sync.dma_start(out=keys_pool[:].bitcast(I32), in_=words_view(keys_words))
+        nc.sync.dma_start(out=gout_raw[:], in_=gout.rearrange("(p j) q -> p j q", j=PACK))
+        nc.sync.dma_start(out=old_sb[:], in_=old)
+
+        nc.vector.memset(gf[:], 0.0)
+        nc.vector.memset(keys_pool_plane[:].bitcast(I32), 0)
+        load_scale_rows(nc.scalar, keys_pool_plane, keys_scales)
+
+        w1_grouped = [sb.tile([P, 2, P, PACK], BF16, name="w1_grouped%d" % u, align_bytes=64) for u in range(2)]
+
+        def w1_views(u, h):
+            dealt = w1_grouped[u][:].rearrange("p t m j -> p m t j")[:, h * (P // 2) : (h + 1) * (P // 2)]
+            src = w1_raw[h][:].rearrange("p j (m t) -> p m t j", t=PACK)[:, :, 2 * u : 2 * u + 2]
+            return dealt, src
+
+        for h in range(2):
+            dealt, src = w1_views(0, h)
+            nc.scalar.copy(out=dealt, in_=src)
         tab_plane = sb.tile([P, I], U8, name="tab_plane", align_bytes=64)
         nc.vector.tensor_copy(out=tab_plane[:], in_=tab_pool_plane[:].indirect(offsets[:]))
-        keys_pool = sb.tile([P, T], U32, name="keys_pool", tag="tab_plane_then_keys")
-        nc.sync.dma_start(out=keys_pool[:].bitcast(I32), in_=words_view(keys_words))
-        nc.vector.tensor_copy(out=dealt[:, P // 2 : P], in_=w1_src[1])
-        w1_mx = quantize("w1", w1_grouped[:].rearrange("p t m j -> p (t m j)"), R)
-        keys_plane = sb.tile([P, I], U8, name="keys_plane", align_bytes=64)
-        nc.vector.tensor_copy(out=keys_plane[:], in_=keys_pool_plane[:].indirect(offsets[:]))
-        gout_raw = sb.tile([P, PACK, Q], F32, name="gout_raw", tag="keys_plane_then_gout")
-        nc.sync.dma_start(out=gout_raw[:], in_=gout.rearrange("(p j) q -> p j q", j=PACK))
-        old_sb = [sb.tile([P, T // 2], F32, name="old_sb%d" % h, tag="w1_then_old%d" % h) for h in range(2)]
         for h in range(2):
-            nc.sync.dma_start(out=old_sb[h][:], in_=old[:, h * (T // 2) : (h + 1) * (T // 2)])
+            dealt, src = w1_views(1, h)
+            nc.vector.tensor_copy(out=dealt, in_=src)
+        w1_mx = {u: quantize("w1_%d" % u, w1_grouped[u][:].rearrange("p t m j -> p (t m j)"), R // 2) for u in (1, 0)}
 
         def gather_half(name, pool, h):
             codes = sb.tile([P, HALF], U32, name="%s_codes%d" % (name, h), align_bytes=64)
@@ -116,6 +124,9 @@ def tile_attend_blrgained_capped_kernel(
             return codes
 
         tab_codes = [gather_half("tab", tab_pool, h) for h in range(2)]
+
+        keys_plane = sb.tile([P, I], U8, name="keys_plane", align_bytes=64)
+        nc.vector.tensor_copy(out=keys_plane[:], in_=keys_pool_plane[:].indirect(offsets[:]))
 
         feature_scale = sb.tile([P, PACK], F32, name="feature_scale")
         nc.vector.tensor_tensor(out=feature_scale[:], in0=gain_sb[:], in1=hsc_sb[:], op=ALU.mult)
@@ -132,7 +143,7 @@ def tile_attend_blrgained_capped_kernel(
             zh = ps.tile([P, PACK, CHUNK], F32, name="zh%d" % c)
             for t in range(PACK):
                 product(
-                    zh[:, t, :], w1_mx, slice(t * P, (t + 1) * P),
+                    zh[:, t, :], w1_mx[t // 2], slice(t % 2 * P, (t % 2 + 1) * P),
                     tab_codes[h][:, lo : lo + CHUNK], tab_plane[:, c * CHUNK : (c + 1) * CHUNK],
                 )
             ht_c = sb.tile([P, CHUNK, PACK], F32, name="ht%d" % c)
@@ -230,7 +241,6 @@ def tile_attend_blrgained_capped_kernel(
 
         for lo in range(0, T, STORE_COLS):
             cols = slice(lo, lo + STORE_COLS)
-            h, at = divmod(lo, T // 2)
             total = sb.tile([P, STORE_COLS], F32, name="total%d" % lo)
-            nc.vector.tensor_tensor(out=total[:], in0=gf[:, cols], in1=old_sb[h][:, at : at + STORE_COLS], op=ALU.add)
+            nc.vector.tensor_tensor(out=total[:], in0=gf[:, cols], in1=old_sb[:, cols], op=ALU.add)
             nc.sync.dma_start(out=out[:, cols], in_=total[:])

@@ -21,7 +21,7 @@ HALF = I // 2
 CHUNK = 128
 OUT_SCALE = 512.0
 LN_FLOOR = 2.0 ** -60
-STORE_COLS = 512
+STORE_WIDTHS = (512, 640, 640, 256)
 
 
 def tile_attend_blrgained_capped_kernel(
@@ -58,47 +58,32 @@ def tile_attend_blrgained_capped_kernel(
             )
 
         offsets = sb.tile([P, I // 16], U16, name="offsets")
-        tab_pool_plane = sb.tile([P, T], U8, name="tab_pool_plane")
-        keys_pool_plane = sb.tile([P, T], U8, name="keys_pool_plane")
+        tab_pool_plane = sb.tile([P, T], U8, name="tab_pool_plane", tag="tab_plane_then_gout")
         gf = sb.tile([P, T], F32, name="gf")
         w1_rows = w1.rearrange("(p j) r -> p j r", j=PACK)
-        w1_raw = [sb.tile([P, PACK, R // 2], F32, name="w1_raw%d" % h) for h in range(2)]
-        tab_pool = sb.tile([P, T], U32, name="tab_pool")
+        w1_raw = [sb.tile([P, PACK, R // 2], F32, name="w1_raw%d" % h, tag="w1_half%d" % h, align_bytes=64) for h in range(2)]
         nc.sync.dma_start(offsets[:], offs)
         for h in range(2):
             nc.sync.dma_start(out=w1_raw[h][:], in_=w1_rows[:, :, h * (R // 2) : (h + 1) * (R // 2)])
-        nc.sync.dma_start(out=tab_pool[:].bitcast(I32), in_=words_view(tab_words))
-        nc.vector.memset(tab_pool_plane[:].bitcast(I32), 0)
-        load_scale_rows(nc.scalar, tab_pool_plane, tab_scales)
-
-        gain_sb = sb.tile([P, PACK], F32, name="gain_sb")
-        hsc_sb = sb.tile([P, PACK], F32, name="hsc_sb")
-        th_sb = sb.tile([P, 1], F32, name="th_sb")
-        reserve_sb = sb.tile([P, 1], F32, name="reserve_sb")
-        nc.gpsimd.dma_start(out=gain_sb[:], in_=gain.rearrange("(p j) o -> p (j o)", j=PACK))
-        nc.gpsimd.dma_start(out=hsc_sb[:], in_=hsc.rearrange("(p j) o -> p (j o)", j=PACK))
-        nc.gpsimd.dma_start(out=th_sb[:], in_=th)
-        nc.gpsimd.dma_start(out=reserve_sb[:], in_=reserve)
+        nc.gpsimd.memset(tab_pool_plane[:].bitcast(I32), 0)
+        load_scale_rows(nc.sync, tab_pool_plane, tab_scales)
 
         with tc.tile_pool(name="head", bufs=1) as head:
             warm = head.tile([P, 1], F32, name="warm")
             warm_out = head.tile([P, 1], F32, name="warm_out")
-            nc.vector.memset(warm[:], 0.0)
+            nc.gpsimd.memset(warm[:], 0.0)
             nc.scalar.activation(out=warm_out[:], in_=warm[:], func=ACT.Sigmoid)
 
-        late = ctx.enter_context(tc.tile_pool(name="late", bufs=1))
-        query_raw = late.tile([P, PACK, Q], F32, name="query_raw")
-        keys_pool = late.tile([P, T], U32, name="keys_pool")
-        gout_raw = late.tile([P, PACK, Q], F32, name="gout_raw")
-        old_sb = late.tile([P, T], F32, name="old_sb")
-        nc.sync.dma_start(out=query_raw[:], in_=query.rearrange("(p j) q -> p j q", j=PACK))
-        nc.sync.dma_start(out=keys_pool[:].bitcast(I32), in_=words_view(keys_words))
-        nc.sync.dma_start(out=gout_raw[:], in_=gout.rearrange("(p j) q -> p j q", j=PACK))
-        nc.sync.dma_start(out=old_sb[:], in_=old)
+        nc.gpsimd.memset(gf[:], 0.0)
 
-        nc.vector.memset(gf[:], 0.0)
+        late = ctx.enter_context(tc.tile_pool(name="late", bufs=1))
+        tab_pool = late.tile([P, T], U32, name="tab_pool", tag="tab_then_old")
+        query_raw = late.tile([P, PACK, Q], F32, name="query_raw")
+        keys_pool_plane = late.tile([P, T], U8, name="keys_pool_plane")
+        nc.sync.dma_start(out=tab_pool[:].bitcast(I32), in_=words_view(tab_words))
+        nc.sync.dma_start(out=query_raw[:], in_=query.rearrange("(p j) q -> p j q", j=PACK))
         nc.vector.memset(keys_pool_plane[:].bitcast(I32), 0)
-        load_scale_rows(nc.scalar, keys_pool_plane, keys_scales)
+        load_scale_rows(nc.sync, keys_pool_plane, keys_scales)
 
         w1_grouped = [sb.tile([P, 2, P, PACK], BF16, name="w1_grouped%d" % u, align_bytes=64) for u in range(2)]
 
@@ -110,11 +95,22 @@ def tile_attend_blrgained_capped_kernel(
         for h in range(2):
             dealt, src = w1_views(0, h)
             nc.scalar.copy(out=dealt, in_=src)
-        tab_plane = sb.tile([P, I], U8, name="tab_plane", align_bytes=64)
-        nc.vector.tensor_copy(out=tab_plane[:], in_=tab_pool_plane[:].indirect(offsets[:]))
         for h in range(2):
             dealt, src = w1_views(1, h)
             nc.vector.tensor_copy(out=dealt, in_=src)
+        tab_plane = sb.tile([P, I], U8, name="tab_plane", align_bytes=64)
+        nc.vector.tensor_copy(out=tab_plane[:], in_=tab_pool_plane[:].indirect(offsets[:]))
+        keys_pool = sb.tile([P, T], U32, name="keys_pool", tag="w1_half0", align_bytes=64)
+        vectors = sb.tile([P, 4, 8], F32, name="vectors", tag="w1_half1", align_bytes=64)
+        gain_sb, hsc_sb = vectors[:, 0, 0:PACK], vectors[:, 1, 0:PACK]
+        th_sb, reserve_sb = vectors[:, 2, 0:1], vectors[:, 3, 0:1]
+        gout_raw = sb.tile([P, PACK, Q], F32, name="gout_raw", tag="tab_plane_then_gout")
+        nc.sync.dma_start(out=keys_pool[:].bitcast(I32), in_=words_view(keys_words))
+        nc.sync.dma_start(out=gain_sb, in_=gain.rearrange("(p j) o -> p (j o)", j=PACK))
+        nc.sync.dma_start(out=hsc_sb, in_=hsc.rearrange("(p j) o -> p (j o)", j=PACK))
+        nc.sync.dma_start(out=th_sb, in_=th)
+        nc.sync.dma_start(out=reserve_sb, in_=reserve)
+        nc.sync.dma_start(out=gout_raw[:], in_=gout.rearrange("(p j) q -> p j q", j=PACK))
         w1_mx = {u: quantize("w1_%d" % u, w1_grouped[u][:].rearrange("p t m j -> p (t m j)"), R // 2) for u in (1, 0)}
 
         def gather_half(name, pool, h):
@@ -129,16 +125,15 @@ def tile_attend_blrgained_capped_kernel(
         nc.vector.tensor_copy(out=keys_plane[:], in_=keys_pool_plane[:].indirect(offsets[:]))
 
         feature_scale = sb.tile([P, PACK], F32, name="feature_scale")
-        nc.vector.tensor_tensor(out=feature_scale[:], in0=gain_sb[:], in1=hsc_sb[:], op=ALU.mult)
+        nc.gpsimd.tensor_tensor(out=feature_scale[:], in0=gain_sb, in1=hsc_sb, op=ALU.mult)
 
         query_grouped = sb.tile([P, Q, PACK], BF16, name="query_grouped", align_bytes=64)
         nc.scalar.activation(
             out=query_grouped[:], in_=query_raw[:].rearrange("p j q -> p q j"), func=ACT.Copy, scale=-1.0
         )
 
-        n_chunks = I // CHUNK
-        ht = []
-        for c in range(n_chunks):
+        ht = [sb.tile([P, HALF, PACK], F32, name="ht%d" % h) for h in range(2)]
+        for c in range(I // CHUNK):
             h, lo = divmod(c * CHUNK, HALF)
             zh = ps.tile([P, PACK, CHUNK], F32, name="zh%d" % c)
             for t in range(PACK):
@@ -146,59 +141,51 @@ def tile_attend_blrgained_capped_kernel(
                     zh[:, t, :], w1_mx[t // 2], slice(t % 2 * P, (t % 2 + 1) * P),
                     tab_codes[h][:, lo : lo + CHUNK], tab_plane[:, c * CHUNK : (c + 1) * CHUNK],
                 )
-            ht_c = sb.tile([P, CHUNK, PACK], F32, name="ht%d" % c)
-            nc.scalar.activation(out=ht_c[:], in_=zh[:].rearrange("p t i -> p i t"), func=ACT.Tanh)
-            ht.append(ht_c)
+            nc.scalar.activation(out=ht[h][:, lo : lo + CHUNK, :], in_=zh[:].rearrange("p t i -> p i t"), func=ACT.Tanh)
 
         query_mx = quantize("query", query_grouped[:].rearrange("p q j -> p (q j)"), Q)
-
-        hs1 = [sb.tile([P, CHUNK, PACK], BF16, name="hs1_%d" % c, align_bytes=64) for c in range(n_chunks)]
-
-        def scale_features(c):
-            nc.vector.tensor_tensor(
-                out=hs1[c][:], in0=ht[c][:], in1=feature_scale[:].unsqueeze(1).to_broadcast([P, CHUNK, PACK]), op=ALU.mult
-            )
-
-        scale_features(0)
         keys_codes = [gather_half("keys", keys_pool, h) for h in range(2)]
-
-        neg_a = [ps.tile([P, HALF], F32, name="neg_a%d" % h) for h in range(2)]
-        sig_neg = sb.tile([P, I], F32, name="sig_neg")
-        for h in range(2):
-            cols = slice(h * HALF, (h + 1) * HALF)
-            product(neg_a[h][:], query_mx, slice(0, Q), keys_codes[h][:], keys_plane[:, cols])
-            nc.scalar.activation(out=sig_neg[:, cols], in_=neg_a[h][:], func=ACT.Sigmoid, bias=th_sb[:])
+        old_sb = late.tile([P, T], F32, name="old_sb", tag="tab_then_old")
+        nc.sync.dma_start(out=old_sb[:], in_=old)
 
         gout_grouped = sb.tile([P, Q, PACK], BF16, name="gout_grouped", align_bytes=64)
-        nc.vector.tensor_copy(out=gout_grouped[:], in_=gout_raw[:].rearrange("p j q -> p q j"))
-        scale_features(1)
-        gout_mx = quantize("gout", gout_grouped[:].rearrange("p q j -> p (q j)"), Q)
+        nc.scalar.copy(out=gout_grouped[:], in_=gout_raw[:].rearrange("p j q -> p q j"))
 
-        c0 = [ps.tile([P, HALF], F32, name="c0_%d" % h) for h in range(2)]
-
-        def read_gradient(c):
-            h, lo = divmod(c * CHUNK, HALF)
-            codes, plane = quantize("hs1_%d" % c, hs1[c][:].rearrange("p i t -> p (i t)"), CHUNK)
-            product(c0[h][:, lo : lo + CHUNK], gout_mx, slice(0, Q), codes[:], plane[:])
-
-        read_gradient(0)
-        for c in range(2, n_chunks):
-            scale_features(c)
-            read_gradient(c - 1)
-        read_gradient(n_chunks - 1)
-
-        ln_sig = sb.tile([P, I], F32, name="ln_sig")
-        neg_p = sb.tile([P, I], F32, name="neg_p")
-        neg_p_sum = [sb.tile([P, 1], F32, name="neg_p_sum%d" % h) for h in range(2)]
+        neg_a = ps.tile([P, I], F32, name="neg_a")
+        sig_neg = sb.tile([P, I], F32, name="sig_neg", tag="tab_plane_then_gout")
         for h in range(2):
             cols = slice(h * HALF, (h + 1) * HALF)
-            nc.scalar.activation(out=ln_sig[:, cols], in_=sig_neg[:, cols], func=ACT.Ln, bias=LN_FLOOR)
-            nc.vector.scalar_tensor_tensor(
-                out=neg_p[:, cols], in0=neg_a[h][:], scalar=th_sb[:], in1=ln_sig[:, cols],
-                op0=ALU.add, op1=ALU.min, accum_out=neg_p_sum[h][:],
-            )
+            product(neg_a[:, cols], query_mx, slice(0, Q), keys_codes[h][:], keys_plane[:, cols])
+        nc.scalar.activation(out=sig_neg[:], in_=neg_a[:], func=ACT.Sigmoid, bias=th_sb)
+        ln_sig = sb.tile([P, I], F32, name="ln_sig")
+        nc.scalar.activation(out=ln_sig[:], in_=sig_neg[:], func=ACT.Ln, bias=LN_FLOOR)
         neg_slope = sb.tile([P, I], F32, name="neg_slope")
         nc.scalar.activation(out=neg_slope[:], in_=sig_neg[:], func=ACT.Copy, scale=OUT_SCALE, bias=-OUT_SCALE)
+
+        hs1_all = sb.tile([P, I * PACK], BF16, name="hs1_all", tag="w1_half0", align_bytes=64)
+        hs1 = [hs1_all[:, h * HALF * PACK : (h + 1) * HALF * PACK] for h in range(2)]
+        c0 = [ps.tile([P, HALF], F32, name="c0_%d" % h) for h in range(2)]
+
+        def scale_features(h):
+            nc.vector.tensor_tensor(
+                out=hs1[h].rearrange("p (i t) -> p i t", t=PACK), in0=ht[h][:], in1=feature_scale[:].unsqueeze(1).to_broadcast([P, HALF, PACK]), op=ALU.mult
+            )
+
+        def read_gradient(h):
+            codes, plane = quantize("hs1_%d" % h, hs1[h], HALF)
+            product(c0[h][:], gout_mx, slice(0, Q), codes[:], plane[:])
+
+        scale_features(0)
+        gout_mx = quantize("gout", gout_grouped[:].rearrange("p q j -> p (q j)"), Q)
+        scale_features(1)
+        read_gradient(0)
+        read_gradient(1)
+
+        neg_p = sb.tile([P, I], F32, name="neg_p")
+        neg_p_sum = sb.tile([P, 1], F32, name="neg_p_sum")
+        nc.vector.scalar_tensor_tensor(
+            out=neg_p[:], in0=neg_a[:], scalar=th_sb, in1=ln_sig[:], op0=ALU.add, op1=ALU.min, accum_out=neg_p_sum[:]
+        )
 
         neg_z = sb.tile([P, 1], F32, name="neg_z")
         neg_rz = sb.tile([P, 1], F32, name="neg_rz")
@@ -214,15 +201,13 @@ def tile_attend_blrgained_capped_kernel(
                 op0=ALU.mult, op1=ALU.mult, accum_out=weighted_sum[h][:],
             )
 
-        nc.vector.tensor_scalar(
-            out=neg_z[:], in0=neg_p_sum[0][:], scalar1=neg_p_sum[1][:], scalar2=reserve_sb[:], op0=ALU.add, op1=ALU.subtract
-        )
+        nc.vector.tensor_tensor(out=neg_z[:], in0=neg_p_sum[:], in1=reserve_sb, op=ALU.subtract)
         weigh(0)
         nc.vector.reciprocal(out=neg_rz[:], in_=neg_z[:])
+        weigh(1)
         nc.vector.tensor_scalar(
             out=neg_rz2[:], in0=neg_rz[:], scalar1=neg_rz[:], scalar2=-1.0, op0=ALU.mult, op1=ALU.mult
         )
-        weigh(1)
         nc.vector.tensor_scalar(
             out=neg_dz[:], in0=weighted_sum[0][:], scalar1=weighted_sum[1][:], scalar2=neg_rz2[:], op0=ALU.add, op1=ALU.mult
         )
@@ -239,8 +224,10 @@ def tile_attend_blrgained_capped_kernel(
                 in0=neg_dp[h][:], in1=neg_slope[:, h * HALF : (h + 1) * HALF], op=ALU.mult,
             )
 
-        for lo in range(0, T, STORE_COLS):
-            cols = slice(lo, lo + STORE_COLS)
-            total = sb.tile([P, STORE_COLS], F32, name="total%d" % lo)
+        lo = 0
+        for width in STORE_WIDTHS:
+            cols = slice(lo, lo + width)
+            total = sb.tile([P, width], F32, name="total%d" % lo)
             nc.vector.tensor_tensor(out=total[:], in0=gf[:, cols], in1=old_sb[:, cols], op=ALU.add)
             nc.sync.dma_start(out=out[:, cols], in_=total[:])
+            lo = lo + width

@@ -17,10 +17,14 @@ ACT = mybir.ActivationFunctionType
 
 P = 128
 PACK = 4
+QUADRANT = 32
+LIST_ROWS = 16
+MX_ALIGN = 64
 HALF = I // 2
 CHUNK = 128
+VECTOR_PAD = 8
 OUT_SCALE = 512.0
-LN_FLOOR = 2.0 ** -60
+FLOOR_ARGUMENT = -40.0
 STORE_WIDTHS = (512, 640, 640, 256)
 
 
@@ -32,104 +36,113 @@ def tile_attend_blrgained_capped_kernel(
         sb = ctx.enter_context(tc.tile_pool(name="sb", bufs=1))
         ps = ctx.enter_context(tc.psum_pool(name="ps", bufs=1))
 
-        def load_scale_rows(engine, plane, scales):
-            rows = scales[0].rearrange("(g f) c -> f g c", f=4)
+        def load_scale_rows(plane, scales):
+            rows = scales[0].rearrange("(quadrant f) c -> f quadrant c", f=4)
             for f in range(4):
-                engine.dma_start(out=plane[f:P:32, :].bitcast(I32), in_=rows[f].bitcast(I32))
+                nc.sync.dma_start(out=plane[f:P:QUADRANT, :].bitcast(I32), in_=rows[f].bitcast(I32))
 
-        def words_view(words):
-            return words[0].rearrange("p n t -> p (n t)").bitcast(I32)
+        def load_words(pool, words):
+            nc.sync.dma_start(out=pool[:].bitcast(I32), in_=words[0].rearrange("p n j -> p (n j)").bitcast(I32))
+
+        def list_half(h):
+            return offsets[:, h * HALF // LIST_ROWS : (h + 1) * HALF // LIST_ROWS]
+
+        def gather_plane(name, pool_plane):
+            plane = sb.tile([P, I], U8, name=name + "_plane", align_bytes=MX_ALIGN)
+            nc.vector.tensor_copy(out=plane[:], in_=pool_plane[:].indirect(offsets[:]))
+            return plane
+
+        def gather_words(name, pool, h):
+            codes = sb.tile([P, HALF], U32, name="%s_codes%d" % (name, h), align_bytes=MX_ALIGN)
+            nc.vector.tensor_copy(out=codes[:], in_=pool[:].indirect(list_half(h)))
+            return codes
 
         def quantize(name, grouped, width):
-            codes = sb.tile([P, width], U32, name=name + "_codes", align_bytes=64)
-            plane = sb.tile([P, width], U8, name=name + "_plane", align_bytes=64)
+            codes = sb.tile([P, width], U32, name=name + "_codes", align_bytes=MX_ALIGN)
+            plane = sb.tile([P, width], U8, name=name + "_plane", align_bytes=MX_ALIGN)
             nc.vector.quantize_mx(out=codes[:].bitcast(FP8X4), scales=plane[:], in_=grouped)
             return codes, plane
 
         def product(acc, lhs, lhs_cols, rhs_codes, rhs_plane):
+            lhs_codes, lhs_plane = lhs
             nc.tensor.matmul_mx(
                 out=acc,
-                lhsT=lhs[0][:, lhs_cols].bitcast(FP8X4),
-                lhsT_scale=lhs[1][:, lhs_cols],
+                lhsT=lhs_codes[:, lhs_cols].bitcast(FP8X4),
+                lhsT_scale=lhs_plane[:, lhs_cols],
                 rhs=rhs_codes.bitcast(FP8X4),
                 rhs_scale=rhs_plane,
                 start=True,
                 stop=True,
             )
 
-        offsets = sb.tile([P, I // 16], U16, name="offsets")
-        tab_pool_plane = sb.tile([P, T], U8, name="tab_pool_plane", tag="tab_plane_then_gout")
+        offsets = sb.tile([P, I // LIST_ROWS], U16, name="offsets")
+        tab_pool_plane = sb.tile([P, T], U8, name="tab_pool_plane", tag="tab_plane_vectors")
         gf = sb.tile([P, T], F32, name="gf")
         w1_rows = w1.rearrange("(p j) r -> p j r", j=PACK)
-        w1_raw = [sb.tile([P, PACK, R // 2], F32, name="w1_raw%d" % h, tag="w1_half%d" % h, align_bytes=64) for h in range(2)]
+        w1_tags = ("w1_keys_hs1", "w1_gout_sigmoid")
+        w1_raw = [
+            sb.tile([P, PACK, R // 2], F32, name="w1_raw%d" % h, tag=w1_tags[h], align_bytes=MX_ALIGN) for h in range(2)
+        ]
         nc.sync.dma_start(offsets[:], offs)
         for h in range(2):
             nc.sync.dma_start(out=w1_raw[h][:], in_=w1_rows[:, :, h * (R // 2) : (h + 1) * (R // 2)])
         nc.gpsimd.memset(tab_pool_plane[:].bitcast(I32), 0)
-        load_scale_rows(nc.sync, tab_pool_plane, tab_scales)
+        load_scale_rows(tab_pool_plane, tab_scales)
 
+        floor = sb.tile([P, 1], F32, name="floor")
         with tc.tile_pool(name="head", bufs=1) as head:
-            warm = head.tile([P, 1], F32, name="warm")
-            warm_out = head.tile([P, 1], F32, name="warm_out")
-            nc.gpsimd.memset(warm[:], 0.0)
-            nc.scalar.activation(out=warm_out[:], in_=warm[:], func=ACT.Sigmoid)
+            floor_argument = head.tile([P, 1], F32, name="floor_argument")
+            nc.gpsimd.memset(floor_argument[:], FLOOR_ARGUMENT)
+            nc.scalar.activation(out=floor[:], in_=floor_argument[:], func=ACT.Sigmoid)
 
         nc.gpsimd.memset(gf[:], 0.0)
 
         late = ctx.enter_context(tc.tile_pool(name="late", bufs=1))
-        tab_pool = late.tile([P, T], U32, name="tab_pool", tag="tab_then_old")
+        tab_pool = late.tile([P, T], U32, name="tab_pool", tag="tab_old")
         query_raw = late.tile([P, PACK, Q], F32, name="query_raw")
         keys_pool_plane = late.tile([P, T], U8, name="keys_pool_plane")
-        nc.sync.dma_start(out=tab_pool[:].bitcast(I32), in_=words_view(tab_words))
+        load_words(tab_pool, tab_words)
         nc.sync.dma_start(out=query_raw[:], in_=query.rearrange("(p j) q -> p j q", j=PACK))
         nc.vector.memset(keys_pool_plane[:].bitcast(I32), 0)
-        load_scale_rows(nc.sync, keys_pool_plane, keys_scales)
+        load_scale_rows(keys_pool_plane, keys_scales)
 
-        w1_grouped = [sb.tile([P, 2, P, PACK], BF16, name="w1_grouped%d" % u, align_bytes=64) for u in range(2)]
+        w1_grouped = [
+            sb.tile([P, 2, P, PACK], BF16, name="w1_grouped%d" % pair, align_bytes=MX_ALIGN) for pair in range(2)
+        ]
+        for pair, cast in enumerate((nc.scalar.copy, nc.vector.tensor_copy)):
+            dealt = w1_grouped[pair][:].rearrange("p t m j -> p m t j")
+            for h in range(2):
+                cast(
+                    out=dealt[:, h * (P // 2) : (h + 1) * (P // 2)],
+                    in_=w1_raw[h][:].rearrange("p j (m t) -> p m t j", t=PACK)[:, :, 2 * pair : 2 * pair + 2],
+                )
+        tab_plane = gather_plane("tab", tab_pool_plane)
 
-        def w1_views(u, h):
-            dealt = w1_grouped[u][:].rearrange("p t m j -> p m t j")[:, h * (P // 2) : (h + 1) * (P // 2)]
-            src = w1_raw[h][:].rearrange("p j (m t) -> p m t j", t=PACK)[:, :, 2 * u : 2 * u + 2]
-            return dealt, src
-
-        for h in range(2):
-            dealt, src = w1_views(0, h)
-            nc.scalar.copy(out=dealt, in_=src)
-        for h in range(2):
-            dealt, src = w1_views(1, h)
-            nc.vector.tensor_copy(out=dealt, in_=src)
-        tab_plane = sb.tile([P, I], U8, name="tab_plane", align_bytes=64)
-        nc.vector.tensor_copy(out=tab_plane[:], in_=tab_pool_plane[:].indirect(offsets[:]))
-        keys_pool = sb.tile([P, T], U32, name="keys_pool", tag="w1_half0", align_bytes=64)
-        vectors = sb.tile([P, 4, 8], F32, name="vectors", tag="w1_half1", align_bytes=64)
+        keys_pool = sb.tile([P, T], U32, name="keys_pool", tag="w1_keys_hs1", align_bytes=MX_ALIGN)
+        vectors = sb.tile([P, 4, VECTOR_PAD], F32, name="vectors", tag="tab_plane_vectors")
         gain_sb, hsc_sb = vectors[:, 0, 0:PACK], vectors[:, 1, 0:PACK]
         th_sb, reserve_sb = vectors[:, 2, 0:1], vectors[:, 3, 0:1]
-        gout_raw = sb.tile([P, PACK, Q], F32, name="gout_raw", tag="tab_plane_then_gout")
-        nc.sync.dma_start(out=keys_pool[:].bitcast(I32), in_=words_view(keys_words))
+        gout_raw = sb.tile([P, PACK, Q], F32, name="gout_raw", tag="w1_gout_sigmoid", align_bytes=MX_ALIGN)
+        load_words(keys_pool, keys_words)
+        nc.sync.dma_start(out=gout_raw[:], in_=gout.rearrange("(p j) q -> p j q", j=PACK))
         nc.sync.dma_start(out=gain_sb, in_=gain.rearrange("(p j) o -> p (j o)", j=PACK))
         nc.sync.dma_start(out=hsc_sb, in_=hsc.rearrange("(p j) o -> p (j o)", j=PACK))
         nc.sync.dma_start(out=th_sb, in_=th)
         nc.sync.dma_start(out=reserve_sb, in_=reserve)
-        nc.sync.dma_start(out=gout_raw[:], in_=gout.rearrange("(p j) q -> p j q", j=PACK))
-        w1_mx = {u: quantize("w1_%d" % u, w1_grouped[u][:].rearrange("p t m j -> p (t m j)"), R // 2) for u in (1, 0)}
 
-        def gather_half(name, pool, h):
-            codes = sb.tile([P, HALF], U32, name="%s_codes%d" % (name, h), align_bytes=64)
-            cols = HALF // 16
-            nc.vector.tensor_copy(out=codes[:], in_=pool[:].indirect(offsets[:, h * cols : (h + 1) * cols]))
-            return codes
-
-        tab_codes = [gather_half("tab", tab_pool, h) for h in range(2)]
-
-        keys_plane = sb.tile([P, I], U8, name="keys_plane", align_bytes=64)
-        nc.vector.tensor_copy(out=keys_plane[:], in_=keys_pool_plane[:].indirect(offsets[:]))
+        w1_mx = {
+            pair: quantize("w1_%d" % pair, w1_grouped[pair][:].rearrange("p t m j -> p (t m j)"), R // 2)
+            for pair in (1, 0)
+        }
+        tab_codes = [gather_words("tab", tab_pool, h) for h in range(2)]
+        keys_plane = gather_plane("keys", keys_pool_plane)
 
         feature_scale = sb.tile([P, PACK], F32, name="feature_scale")
         nc.gpsimd.tensor_tensor(out=feature_scale[:], in0=gain_sb, in1=hsc_sb, op=ALU.mult)
 
-        query_grouped = sb.tile([P, Q, PACK], BF16, name="query_grouped", align_bytes=64)
+        neg_query_grouped = sb.tile([P, Q, PACK], BF16, name="neg_query_grouped", align_bytes=MX_ALIGN)
         nc.scalar.activation(
-            out=query_grouped[:], in_=query_raw[:].rearrange("p j q -> p q j"), func=ACT.Copy, scale=-1.0
+            out=neg_query_grouped[:], in_=query_raw[:].rearrange("p j q -> p q j"), func=ACT.Copy, scale=-1.0
         )
 
         ht = [sb.tile([P, HALF, PACK], F32, name="ht%d" % h) for h in range(2)]
@@ -137,97 +150,90 @@ def tile_attend_blrgained_capped_kernel(
             h, lo = divmod(c * CHUNK, HALF)
             zh = ps.tile([P, PACK, CHUNK], F32, name="zh%d" % c)
             for t in range(PACK):
+                pair, place = divmod(t, 2)
                 product(
-                    zh[:, t, :], w1_mx[t // 2], slice(t % 2 * P, (t % 2 + 1) * P),
-                    tab_codes[h][:, lo : lo + CHUNK], tab_plane[:, c * CHUNK : (c + 1) * CHUNK],
+                    zh[:, t, :],
+                    w1_mx[pair],
+                    slice(place * P, (place + 1) * P),
+                    tab_codes[h][:, lo : lo + CHUNK],
+                    tab_plane[:, c * CHUNK : (c + 1) * CHUNK],
                 )
             nc.scalar.activation(out=ht[h][:, lo : lo + CHUNK, :], in_=zh[:].rearrange("p t i -> p i t"), func=ACT.Tanh)
 
-        query_mx = quantize("query", query_grouped[:].rearrange("p q j -> p (q j)"), Q)
-        keys_codes = [gather_half("keys", keys_pool, h) for h in range(2)]
-        old_sb = late.tile([P, T], F32, name="old_sb", tag="tab_then_old")
+        neg_query_mx = quantize("neg_query", neg_query_grouped[:].rearrange("p q j -> p (q j)"), Q)
+        keys_codes = [gather_words("keys", keys_pool, h) for h in range(2)]
+        old_sb = late.tile([P, T], F32, name="old_sb", tag="tab_old")
         nc.sync.dma_start(out=old_sb[:], in_=old)
 
-        gout_grouped = sb.tile([P, Q, PACK], BF16, name="gout_grouped", align_bytes=64)
+        gout_grouped = sb.tile([P, Q, PACK], BF16, name="gout_grouped", align_bytes=MX_ALIGN)
         nc.scalar.copy(out=gout_grouped[:], in_=gout_raw[:].rearrange("p j q -> p q j"))
 
         neg_a = ps.tile([P, I], F32, name="neg_a")
-        sig_neg = sb.tile([P, I], F32, name="sig_neg", tag="tab_plane_then_gout")
+        sig_neg = sb.tile([P, I], F32, name="sig_neg", tag="w1_gout_sigmoid", align_bytes=MX_ALIGN)
         for h in range(2):
-            cols = slice(h * HALF, (h + 1) * HALF)
-            product(neg_a[:, cols], query_mx, slice(0, Q), keys_codes[h][:], keys_plane[:, cols])
-        nc.scalar.activation(out=sig_neg[:], in_=neg_a[:], func=ACT.Sigmoid, bias=th_sb)
+            slots = slice(h * HALF, (h + 1) * HALF)
+            product(neg_a[:, slots], neg_query_mx, slice(0, Q), keys_codes[h][:], keys_plane[:, slots])
+            nc.scalar.activation(out=sig_neg[:, slots], in_=neg_a[:, slots], func=ACT.Sigmoid, bias=th_sb)
         ln_sig = sb.tile([P, I], F32, name="ln_sig")
-        nc.scalar.activation(out=ln_sig[:], in_=sig_neg[:], func=ACT.Ln, bias=LN_FLOOR)
-        neg_slope = sb.tile([P, I], F32, name="neg_slope")
-        nc.scalar.activation(out=neg_slope[:], in_=sig_neg[:], func=ACT.Copy, scale=OUT_SCALE, bias=-OUT_SCALE)
+        nc.scalar.activation(out=ln_sig[:], in_=sig_neg[:], func=ACT.Ln, bias=floor[:])
+        slope = sb.tile([P, I], F32, name="slope")
+        nc.scalar.activation(out=slope[:], in_=sig_neg[:], func=ACT.Copy, scale=-OUT_SCALE, bias=OUT_SCALE)
 
-        hs1_all = sb.tile([P, I * PACK], BF16, name="hs1_all", tag="w1_half0", align_bytes=64)
+        hs1_all = sb.tile([P, I * PACK], BF16, name="hs1_all", tag="w1_keys_hs1", align_bytes=MX_ALIGN)
         hs1 = [hs1_all[:, h * HALF * PACK : (h + 1) * HALF * PACK] for h in range(2)]
-        c0 = [ps.tile([P, HALF], F32, name="c0_%d" % h) for h in range(2)]
+        c0 = ps.tile([P, I], F32, name="c0")
 
         def scale_features(h):
             nc.vector.tensor_tensor(
-                out=hs1[h].rearrange("p (i t) -> p i t", t=PACK), in0=ht[h][:], in1=feature_scale[:].unsqueeze(1).to_broadcast([P, HALF, PACK]), op=ALU.mult
+                out=hs1[h].rearrange("p (i t) -> p i t", t=PACK),
+                in0=ht[h][:],
+                in1=feature_scale[:].unsqueeze(1).to_broadcast([P, HALF, PACK]),
+                op=ALU.mult,
             )
 
         def read_gradient(h):
             codes, plane = quantize("hs1_%d" % h, hs1[h], HALF)
-            product(c0[h][:], gout_mx, slice(0, Q), codes[:], plane[:])
+            product(c0[:, h * HALF : (h + 1) * HALF], gout_mx, slice(0, Q), codes[:], plane[:])
 
         scale_features(0)
         gout_mx = quantize("gout", gout_grouped[:].rearrange("p q j -> p (q j)"), Q)
         scale_features(1)
         read_gradient(0)
-        read_gradient(1)
 
         neg_p = sb.tile([P, I], F32, name="neg_p")
         neg_p_sum = sb.tile([P, 1], F32, name="neg_p_sum")
+        z = sb.tile([P, 1], F32, name="z")
+        rz = sb.tile([P, 1], F32, name="rz")
         nc.vector.scalar_tensor_tensor(
             out=neg_p[:], in0=neg_a[:], scalar=th_sb, in1=ln_sig[:], op0=ALU.add, op1=ALU.min, accum_out=neg_p_sum[:]
         )
+        nc.scalar.activation(out=z[:], in_=neg_p_sum[:], func=ACT.Identity, scale=-1.0, bias=reserve_sb)
+        read_gradient(1)
+        nc.vector.reciprocal(out=rz[:], in_=z[:])
 
-        neg_z = sb.tile([P, 1], F32, name="neg_z")
-        neg_rz = sb.tile([P, 1], F32, name="neg_rz")
-        neg_rz2 = sb.tile([P, 1], F32, name="neg_rz2")
-        neg_dz = sb.tile([P, 1], F32, name="neg_dz")
-        weighted = sb.tile([P, I], F32, name="weighted")
-        weighted_sum = [sb.tile([P, 1], F32, name="weighted_sum%d" % h) for h in range(2)]
-
-        def weigh(h):
-            cols = slice(h * HALF, (h + 1) * HALF)
-            nc.vector.scalar_tensor_tensor(
-                out=weighted[:, cols], in0=c0[h][:], scalar=1.0, in1=neg_p[:, cols],
-                op0=ALU.mult, op1=ALU.mult, accum_out=weighted_sum[h][:],
-            )
-
-        nc.vector.tensor_tensor(out=neg_z[:], in0=neg_p_sum[:], in1=reserve_sb, op=ALU.subtract)
-        weigh(0)
-        nc.vector.reciprocal(out=neg_rz[:], in_=neg_z[:])
-        weigh(1)
-        nc.vector.tensor_scalar(
-            out=neg_rz2[:], in0=neg_rz[:], scalar1=neg_rz[:], scalar2=-1.0, op0=ALU.mult, op1=ALU.mult
-        )
-        nc.vector.tensor_scalar(
-            out=neg_dz[:], in0=weighted_sum[0][:], scalar1=weighted_sum[1][:], scalar2=neg_rz2[:], op0=ALU.add, op1=ALU.mult
+        terms = sb.tile([P, I], F32, name="terms")
+        dz_z = sb.tile([P, 1], F32, name="dz_z")
+        dz = sb.tile([P, 1], F32, name="dz")
+        nc.vector.scalar_tensor_tensor(
+            out=terms[:], in0=c0[:], scalar=rz[:], in1=neg_p[:], op0=ALU.mult, op1=ALU.mult, accum_out=dz_z[:]
         )
 
-        neg_dp = [sb.tile([P, HALF], F32, name="neg_dp%d" % h) for h in range(2)]
+        dp = [sb.tile([P, HALF], F32, name="dp%d" % h) for h in range(2)]
         nc.vector.tensor_scalar(
-            out=neg_dp[0][:], in0=c0[0][:], scalar1=neg_rz[:], scalar2=neg_dz[:], op0=ALU.mult, op1=ALU.add
+            out=dp[0][:], in0=c0[:, 0:HALF], scalar1=dz_z[:], scalar2=rz[:], op0=ALU.add, op1=ALU.mult
         )
-        nc.scalar.activation(out=neg_dp[1][:], in_=c0[1][:], func=ACT.Identity, scale=neg_rz[:], bias=neg_dz[:])
+        nc.scalar.activation(out=dz[:], in_=dz_z[:], func=ACT.Copy, scale=rz[:])
+        nc.scalar.activation(out=dp[1][:], in_=c0[:, HALF:I], func=ACT.Identity, scale=rz[:], bias=dz[:])
+
         for h in range(2):
-            cols = HALF // 16
             nc.vector.tensor_tensor(
-                out=gf[:].indirect(offsets[:, h * cols : (h + 1) * cols]),
-                in0=neg_dp[h][:], in1=neg_slope[:, h * HALF : (h + 1) * HALF], op=ALU.mult,
+                out=gf[:].indirect(list_half(h)), in0=dp[h][:], in1=slope[:, h * HALF : (h + 1) * HALF], op=ALU.mult
             )
 
-        lo = 0
+        first = 0
         for width in STORE_WIDTHS:
-            cols = slice(lo, lo + width)
-            total = sb.tile([P, width], F32, name="total%d" % lo)
-            nc.vector.tensor_tensor(out=total[:], in0=gf[:, cols], in1=old_sb[:, cols], op=ALU.add)
-            nc.sync.dma_start(out=out[:, cols], in_=total[:])
-            lo = lo + width
+            tokens = slice(first, first + width)
+            total = sb.tile([P, width], F32, name="total%d" % first)
+            nc.vector.tensor_tensor(out=total[:], in0=gf[:, tokens], in1=old_sb[:, tokens], op=ALU.add)
+            nc.sync.dma_start(out=out[:, tokens], in_=total[:])
+            first = first + width

from contextlib import ExitStack

import concourse.mybir as mybir

D, K, R, T, I, Q = 512, 512, 512, 2048, 512, 128
FLOPS = 2 * (D * Q * I + K * R * I + R * Q * I)

F32 = mybir.dt.float32
BF16 = mybir.dt.bfloat16
I32 = mybir.dt.int32
U32 = mybir.dt.uint32
U16 = mybir.dt.uint16
U8 = mybir.dt.uint8
FP8X4 = mybir.dt.float8_e4m3fn_x4
ALU = mybir.AluOpType
ACT = mybir.ActivationFunctionType

P = 128
PACK = 4
QUADRANT = 32
LIST_ROWS = 16
MX_ALIGN = 64
HALF = I // 2
CHUNK = 128
VECTOR_PAD = 8
OUT_SCALE = 512.0
FLOOR_ARGUMENT = -40.0
STORE_WIDTHS = (512, 640, 640, 256)


def tile_attend_blrgained_capped_kernel(
    tc, query, keys_words, keys_scales, th, reserve, tab_words, tab_scales, w1, gain, gout, hsc, old, offs, out
):
    nc = tc.nc
    with ExitStack() as ctx:
        sb = ctx.enter_context(tc.tile_pool(name="sb", bufs=1))
        ps = ctx.enter_context(tc.psum_pool(name="ps", bufs=1))

        def load_scale_rows(plane, scales):
            rows = scales[0].rearrange("(quadrant f) c -> f quadrant c", f=4)
            for f in range(4):
                nc.sync.dma_start(out=plane[f:P:QUADRANT, :].bitcast(I32), in_=rows[f].bitcast(I32))

        def load_words(pool, words):
            nc.sync.dma_start(out=pool[:].bitcast(I32), in_=words[0].rearrange("p n j -> p (n j)").bitcast(I32))

        def list_half(h):
            return offsets[:, h * HALF // LIST_ROWS : (h + 1) * HALF // LIST_ROWS]

        def gather_plane(name, pool_plane):
            plane = sb.tile([P, I], U8, name=name + "_plane", align_bytes=MX_ALIGN)
            nc.vector.tensor_copy(out=plane[:], in_=pool_plane[:].indirect(offsets[:]))
            return plane

        def gather_words(name, pool, h):
            codes = sb.tile([P, HALF], U32, name="%s_codes%d" % (name, h), align_bytes=MX_ALIGN)
            nc.vector.tensor_copy(out=codes[:], in_=pool[:].indirect(list_half(h)))
            return codes

        def quantize(name, grouped, width):
            codes = sb.tile([P, width], U32, name=name + "_codes", align_bytes=MX_ALIGN)
            plane = sb.tile([P, width], U8, name=name + "_plane", align_bytes=MX_ALIGN)
            nc.vector.quantize_mx(out=codes[:].bitcast(FP8X4), scales=plane[:], in_=grouped)
            return codes, plane

        def product(acc, lhs, lhs_cols, rhs_codes, rhs_plane):
            lhs_codes, lhs_plane = lhs
            nc.tensor.matmul_mx(
                out=acc,
                lhsT=lhs_codes[:, lhs_cols].bitcast(FP8X4),
                lhsT_scale=lhs_plane[:, lhs_cols],
                rhs=rhs_codes.bitcast(FP8X4),
                rhs_scale=rhs_plane,
                start=True,
                stop=True,
            )

        offsets = sb.tile([P, I // LIST_ROWS], U16, name="offsets")
        tab_pool_plane = sb.tile([P, T], U8, name="tab_pool_plane", tag="tab_plane_vectors")
        gf = sb.tile([P, T], F32, name="gf")
        w1_rows = w1.rearrange("(p j) r -> p j r", j=PACK)
        w1_tags = ("w1_keys_hs1", "w1_gout_sigmoid")
        w1_raw = [
            sb.tile([P, PACK, R // 2], F32, name="w1_raw%d" % h, tag=w1_tags[h], align_bytes=MX_ALIGN) for h in range(2)
        ]
        nc.sync.dma_start(offsets[:], offs)
        for h in range(2):
            nc.sync.dma_start(out=w1_raw[h][:], in_=w1_rows[:, :, h * (R // 2) : (h + 1) * (R // 2)])
        nc.gpsimd.memset(tab_pool_plane[:].bitcast(I32), 0)
        load_scale_rows(tab_pool_plane, tab_scales)

        floor = sb.tile([P, 1], F32, name="floor")
        with tc.tile_pool(name="head", bufs=1) as head:
            floor_argument = head.tile([P, 1], F32, name="floor_argument")
            nc.gpsimd.memset(floor_argument[:], FLOOR_ARGUMENT)
            nc.scalar.activation(out=floor[:], in_=floor_argument[:], func=ACT.Sigmoid)

        nc.gpsimd.memset(gf[:], 0.0)

        late = ctx.enter_context(tc.tile_pool(name="late", bufs=1))
        tab_pool = late.tile([P, T], U32, name="tab_pool", tag="tab_old")
        query_raw = late.tile([P, PACK, Q], F32, name="query_raw")
        keys_pool_plane = late.tile([P, T], U8, name="keys_pool_plane")
        load_words(tab_pool, tab_words)
        nc.sync.dma_start(out=query_raw[:], in_=query.rearrange("(p j) q -> p j q", j=PACK))
        nc.vector.memset(keys_pool_plane[:].bitcast(I32), 0)
        load_scale_rows(keys_pool_plane, keys_scales)

        w1_grouped = [
            sb.tile([P, 2, P, PACK], BF16, name="w1_grouped%d" % pair, align_bytes=MX_ALIGN) for pair in range(2)
        ]
        for pair, cast in enumerate((nc.scalar.copy, nc.vector.tensor_copy)):
            dealt = w1_grouped[pair][:].rearrange("p t m j -> p m t j")
            for h in range(2):
                cast(
                    out=dealt[:, h * (P // 2) : (h + 1) * (P // 2)],
                    in_=w1_raw[h][:].rearrange("p j (m t) -> p m t j", t=PACK)[:, :, 2 * pair : 2 * pair + 2],
                )
        tab_plane = gather_plane("tab", tab_pool_plane)

        keys_pool = sb.tile([P, T], U32, name="keys_pool", tag="w1_keys_hs1", align_bytes=MX_ALIGN)
        vectors = sb.tile([P, 4, VECTOR_PAD], F32, name="vectors", tag="tab_plane_vectors")
        gain_sb, hsc_sb = vectors[:, 0, 0:PACK], vectors[:, 1, 0:PACK]
        th_sb, reserve_sb = vectors[:, 2, 0:1], vectors[:, 3, 0:1]
        gout_raw = sb.tile([P, PACK, Q], F32, name="gout_raw", tag="w1_gout_sigmoid", align_bytes=MX_ALIGN)
        load_words(keys_pool, keys_words)
        nc.sync.dma_start(out=gout_raw[:], in_=gout.rearrange("(p j) q -> p j q", j=PACK))
        nc.sync.dma_start(out=gain_sb, in_=gain.rearrange("(p j) o -> p (j o)", j=PACK))
        nc.sync.dma_start(out=hsc_sb, in_=hsc.rearrange("(p j) o -> p (j o)", j=PACK))
        nc.sync.dma_start(out=th_sb, in_=th)
        nc.sync.dma_start(out=reserve_sb, in_=reserve)

        w1_mx = {
            pair: quantize("w1_%d" % pair, w1_grouped[pair][:].rearrange("p t m j -> p (t m j)"), R // 2)
            for pair in (1, 0)
        }
        tab_codes = [gather_words("tab", tab_pool, h) for h in range(2)]
        keys_plane = gather_plane("keys", keys_pool_plane)

        feature_scale = sb.tile([P, PACK], F32, name="feature_scale")
        nc.gpsimd.tensor_tensor(out=feature_scale[:], in0=gain_sb, in1=hsc_sb, op=ALU.mult)

        neg_query_grouped = sb.tile([P, Q, PACK], BF16, name="neg_query_grouped", align_bytes=MX_ALIGN)
        nc.scalar.activation(
            out=neg_query_grouped[:], in_=query_raw[:].rearrange("p j q -> p q j"), func=ACT.Copy, scale=-1.0
        )

        ht = [sb.tile([P, HALF, PACK], F32, name="ht%d" % h) for h in range(2)]
        for c in range(I // CHUNK):
            h, lo = divmod(c * CHUNK, HALF)
            zh = ps.tile([P, PACK, CHUNK], F32, name="zh%d" % c)
            for t in range(PACK):
                pair, place = divmod(t, 2)
                product(
                    zh[:, t, :],
                    w1_mx[pair],
                    slice(place * P, (place + 1) * P),
                    tab_codes[h][:, lo : lo + CHUNK],
                    tab_plane[:, c * CHUNK : (c + 1) * CHUNK],
                )
            nc.scalar.activation(out=ht[h][:, lo : lo + CHUNK, :], in_=zh[:].rearrange("p t i -> p i t"), func=ACT.Tanh)

        neg_query_mx = quantize("neg_query", neg_query_grouped[:].rearrange("p q j -> p (q j)"), Q)
        keys_codes = [gather_words("keys", keys_pool, h) for h in range(2)]
        old_sb = late.tile([P, T], F32, name="old_sb", tag="tab_old")
        nc.sync.dma_start(out=old_sb[:], in_=old)

        gout_grouped = sb.tile([P, Q, PACK], BF16, name="gout_grouped", align_bytes=MX_ALIGN)
        nc.scalar.copy(out=gout_grouped[:], in_=gout_raw[:].rearrange("p j q -> p q j"))

        neg_a = ps.tile([P, I], F32, name="neg_a")
        sig_neg = sb.tile([P, I], F32, name="sig_neg", tag="w1_gout_sigmoid", align_bytes=MX_ALIGN)
        for h in range(2):
            slots = slice(h * HALF, (h + 1) * HALF)
            product(neg_a[:, slots], neg_query_mx, slice(0, Q), keys_codes[h][:], keys_plane[:, slots])
            nc.scalar.activation(out=sig_neg[:, slots], in_=neg_a[:, slots], func=ACT.Sigmoid, bias=th_sb)
        ln_sig = sb.tile([P, I], F32, name="ln_sig")
        nc.scalar.activation(out=ln_sig[:], in_=sig_neg[:], func=ACT.Ln, bias=floor[:])
        slope = sb.tile([P, I], F32, name="slope")
        nc.scalar.activation(out=slope[:], in_=sig_neg[:], func=ACT.Copy, scale=-OUT_SCALE, bias=OUT_SCALE)

        hs1_all = sb.tile([P, I * PACK], BF16, name="hs1_all", tag="w1_keys_hs1", align_bytes=MX_ALIGN)
        hs1 = [hs1_all[:, h * HALF * PACK : (h + 1) * HALF * PACK] for h in range(2)]
        c0 = ps.tile([P, I], F32, name="c0")

        def scale_features(h):
            nc.vector.tensor_tensor(
                out=hs1[h].rearrange("p (i t) -> p i t", t=PACK),
                in0=ht[h][:],
                in1=feature_scale[:].unsqueeze(1).to_broadcast([P, HALF, PACK]),
                op=ALU.mult,
            )

        def read_gradient(h):
            codes, plane = quantize("hs1_%d" % h, hs1[h], HALF)
            product(c0[:, h * HALF : (h + 1) * HALF], gout_mx, slice(0, Q), codes[:], plane[:])

        scale_features(0)
        gout_mx = quantize("gout", gout_grouped[:].rearrange("p q j -> p (q j)"), Q)
        scale_features(1)
        read_gradient(0)

        neg_p = sb.tile([P, I], F32, name="neg_p")
        neg_p_sum = sb.tile([P, 1], F32, name="neg_p_sum")
        z = sb.tile([P, 1], F32, name="z")
        rz = sb.tile([P, 1], F32, name="rz")
        nc.vector.scalar_tensor_tensor(
            out=neg_p[:], in0=neg_a[:], scalar=th_sb, in1=ln_sig[:], op0=ALU.add, op1=ALU.min, accum_out=neg_p_sum[:]
        )
        nc.scalar.activation(out=z[:], in_=neg_p_sum[:], func=ACT.Identity, scale=-1.0, bias=reserve_sb)
        read_gradient(1)
        nc.vector.reciprocal(out=rz[:], in_=z[:])

        terms = sb.tile([P, I], F32, name="terms")
        dz_z = sb.tile([P, 1], F32, name="dz_z")
        dz = sb.tile([P, 1], F32, name="dz")
        nc.vector.scalar_tensor_tensor(
            out=terms[:], in0=c0[:], scalar=rz[:], in1=neg_p[:], op0=ALU.mult, op1=ALU.mult, accum_out=dz_z[:]
        )

        dp = [sb.tile([P, HALF], F32, name="dp%d" % h) for h in range(2)]
        nc.vector.tensor_scalar(
            out=dp[0][:], in0=c0[:, 0:HALF], scalar1=dz_z[:], scalar2=rz[:], op0=ALU.add, op1=ALU.mult
        )
        nc.scalar.activation(out=dz[:], in_=dz_z[:], func=ACT.Copy, scale=rz[:])
        nc.scalar.activation(out=dp[1][:], in_=c0[:, HALF:I], func=ACT.Identity, scale=rz[:], bias=dz[:])

        for h in range(2):
            nc.vector.tensor_tensor(
                out=gf[:].indirect(list_half(h)), in0=dp[h][:], in1=slope[:, h * HALF : (h + 1) * HALF], op=ALU.mult
            )

        first = 0
        for width in STORE_WIDTHS:
            tokens = slice(first, first + width)
            total = sb.tile([P, width], F32, name="total%d" % first)
            nc.vector.tensor_tensor(out=total[:], in0=gf[:, tokens], in1=old_sb[:, tokens], op=ALU.add)
            nc.sync.dma_start(out=out[:, tokens], in_=total[:])
            first = first + width
